import numpy as np
import ml_dtypes


def mxq(x, axis, fmt="e4m3"):
    dtype, down = {"e4m3": (ml_dtypes.float8_e4m3fn, 7), "e5m2": (ml_dtypes.float8_e5m2, 14)}[fmt]
    v = np.moveaxis(np.asarray(x, np.float32).astype(ml_dtypes.bfloat16).astype(np.float64), axis, -1)
    blocks = v.reshape(v.shape[:-1] + (-1, 32))
    amax = np.abs(blocks).max(-1, keepdims=True)
    byte = np.maximum(np.where(amax > 0, np.frexp(amax)[1] - 1 + 127, 0) - down, 1)
    scale = np.exp2(byte - 127.0)
    codes = (blocks / scale).astype(np.float32).astype(dtype).astype(np.float64)
    return np.moveaxis((codes * scale).reshape(v.shape), -1, axis)


WIDE = False


def mx_kscale(k, group=512):
    if not WIDE:
        return np.ones(k)
    levels = np.array([18, -18])
    if group != 512:
        return np.exp2(np.random.permutation(np.resize(levels, k // group))).repeat(group)
    if k % 512:
        return np.exp2(np.random.permutation(np.resize(levels, k // 32))).repeat(32)
    a = np.empty((k // 512, 16))
    for p in range(k // 512):
        a[p, :8] = np.random.permutation(np.resize(levels, 8))
        for g in range(8):
            far = levels[np.abs(levels - a[p, g]) >= 10]
            a[p, g + 8] = far[np.random.randint(len(far))]
    return np.exp2(a.ravel()).repeat(32)


def f64(x):
    return np.asarray(x).astype(np.float64)


def sigmoid(v):
    return 1.0 / (1.0 + np.exp(-v))


def bf(x):
    return np.asarray(x, np.float32).astype(ml_dtypes.bfloat16)


def planes(Y):
    r, m = Y.shape
    b = f64(bf(Y)).reshape(r // 32, 32, m)
    amax = np.abs(b).max(1)
    byte = np.clip(np.where(amax > 0, np.frexp(amax)[1] - 1 + 127 - 7, 1), 1, 254)
    codes = (b * np.exp2(127.0 - byte)[:, None, :]).reshape(r, m).astype(np.float32).astype(ml_dtypes.float8_e4m3fn).view(np.uint8)
    words = codes.reshape(r // 512, 128, 4, m).transpose(0, 1, 3, 2)
    return np.ascontiguousarray(words), np.ascontiguousarray(byte.astype(np.uint8).reshape(r // 512, 16, m))


G, D, M, N = 4, 128, 128, 512


def setup_inputs():
    n = np.random.standard_normal
    s_d = mx_kscale(D, 0)
    return {
        "h": (n((G, D, N)) * s_d[:, None]).astype(np.float32),
        "wi": (n((G, D, M)) / np.sqrt(D) / s_d[:, None]).astype(np.float32),
        "wf": (n((G, D, M)) / np.sqrt(D) / s_d[:, None]).astype(np.float32),
        "wo": (n((G, D, M)) / np.sqrt(D) / s_d[:, None]).astype(np.float32),
        "wc": (n((G, D, M)) / np.sqrt(D) / s_d[:, None]).astype(np.float32),
        "xi": (n((G, M, N))).astype(np.float32),
        "xf": (n((G, M, N))).astype(np.float32),
        "xo": (n((G, M, N))).astype(np.float32),
        "xc": (n((G, M, N))).astype(np.float32),
        "c": (n((G, M, N))).astype(np.float32),
    }


def reference(h, wi, wf, wo, wc, xi, xf, xo, xc, c):
    wiq = mxq(f64(wi), 1, "e4m3")
    hq = mxq(f64(h), 1, "e4m3")
    zi = wiq.transpose(0, 2, 1) @ hq
    wfq = mxq(f64(wf), 1, "e4m3")
    zf = wfq.transpose(0, 2, 1) @ hq
    woq = mxq(f64(wo), 1, "e4m3")
    zo = woq.transpose(0, 2, 1) @ hq
    wcq = mxq(f64(wc), 1, "e4m3")
    zc = wcq.transpose(0, 2, 1) @ hq
    ig = np.exp(0.5 * (zi + f64(xi)))
    cn = sigmoid(zf + f64(xf)) * f64(c) + ig * np.tanh(zc + f64(xc))
    ab = sigmoid(zf + f64(xf)) + ig
    y = sigmoid(zo + f64(xo)) * cn / (ab + 1.0)
    Y = y.reshape(G * M, N)
    words, scales = planes(Y)
    return Y, words, scales

@@ -1,0 +1,286 @@
+import math
+from contextlib import ExitStack
+
+import concourse.mybir as mybir
+
+G, D, M, N = 4, 128, 128, 512
+FLOPS = 2 * 4 * G * D * M * N
+
+F32 = mybir.dt.float32
+BF16 = mybir.dt.bfloat16
+I32 = mybir.dt.int32
+U32 = mybir.dt.uint32
+U8 = mybir.dt.uint8
+FP8X4 = mybir.dt.float8_e4m3fn_x4
+ALU = mybir.AluOpType
+ACT = mybir.ActivationFunctionType
+
+P = 128
+PACK = 4
+ROWS = 32
+RUN = 4
+HALF = N // 2
+QUARTER = N // 4
+
+
+def walk_in(raw):
+    return raw.rearrange("p t (c i) -> p c t i", i=RUN)
+
+
+def walk_out(grouped):
+    return grouped.rearrange("p (c i) t -> p c t i", i=RUN)
+
+
+def quantize(nc, codes, scales, grouped):
+    nc.vector.quantize_mx(
+        out=codes.bitcast(FP8X4), scales=scales, in_=grouped.rearrange("p c t -> p (c t)")
+    )
+
+
+def tile_rows_pl_cell_slstm_kernel(tc, h, wi, wf, wo, wc, xi, xf, xo, xc, c, out_0, out_1, out_2):
+    nc = tc.nc
+    heads = range(G)
+    with ExitStack() as ctx:
+        sb = ctx.enter_context(tc.tile_pool(name="sb", bufs=1))
+        psum = ctx.enter_context(tc.psum_pool(name="psum", bufs=1))
+        ctx.enter_context(tc.manual_schedule())
+
+        def per_head(name):
+            return [sb.tile([P, N], F32, name="%s%d" % (name, g)) for g in heads]
+
+        bank_a = [psum.tile([M, N], F32, name="bank_a%d" % g) for g in heads]
+        bank_b = [psum.tile([M, N], F32, name="bank_b%d" % g) for g in heads]
+
+        w_dram = {"f": wf, "c": wc, "o": wo, "i": wi}
+        w_raw = {k: sb.tile([P, PACK, M], F32, name="w_raw_" + k) for k in w_dram}
+        w_bf = {k: sb.tile([P, M, PACK], BF16, name="w_bf_" + k, align_bytes=64) for k in w_dram}
+        w_codes = {k: sb.tile([P, M], U32, name="w_codes_" + k, align_bytes=64) for k in w_dram}
+        w_scales = {k: sb.tile([P, M], U8, name="w_scales_" + k, align_bytes=64) for k in w_dram}
+        h_raw = [sb.tile([P, PACK, HALF], F32, name="h_raw%d" % u) for u in range(2)]
+        h_bf = [sb.tile([P, HALF, PACK], BF16, name="h_bf%d" % u, align_bytes=64) for u in range(2)]
+        h_codes = sb.tile([P, N], U32, align_bytes=64)
+        h_scales = sb.tile([P, N], U8, align_bytes=64)
+
+        x_dram = {"f": xf, "c": xc, "o": xo, "i": xi, "cell": c}
+        x_sb = {k: per_head("x_" + k) for k in x_dram}
+        pre_f, pre_c, pre_o = per_head("pre_f"), per_head("pre_c"), per_head("pre_o")
+        forget, log_k, beta = per_head("forget"), per_head("log_k"), per_head("beta")
+        cand, out_gate = per_head("cand"), per_head("out_gate")
+        part_i, pre_a, alpha = per_head("part_i"), per_head("pre_a"), per_head("alpha")
+        kept, diff, step, mixed, y = (per_head(n) for n in ("kept", "diff", "step", "mixed", "y"))
+        y_dealt = [sb.tile([P, PACK, QUARTER], F32, name="y_dealt%d" % g) for g in heads]
+        y_bf = [sb.tile([P, QUARTER, PACK], BF16, name="y_bf%d" % g, align_bytes=64) for g in heads]
+        y_codes = [sb.tile([P, QUARTER], U32, name="y_codes%d" % g, align_bytes=64) for g in heads]
+        y_scales = sb.tile([P, G, QUARTER], U8, align_bytes=64)
+
+        def load_w(k):
+            nc.sync.dma_start(out=w_raw[k][:], in_=w_dram[k].rearrange("g (p t) m -> (g p) t m", t=PACK))
+
+        def load_x(k, g):
+            nc.sync.dma_start(out=x_sb[k][g][:], in_=x_dram[k][g])
+
+        h_rows = h.rearrange("g (p t) n -> (g p) t n", t=PACK)
+        load_w("f")
+        for u in range(2):
+            nc.sync.dma_start(out=h_raw[u][:], in_=h_rows[:, :, u * HALF : (u + 1) * HALF])
+        for k_w, k_x in (("c", "f"), ("o", "c"), ("i", "o")):
+            load_w(k_w)
+            for g in heads:
+                load_x(k_x, g)
+        load_x("i", 0)
+        for g in heads:
+            if g + 1 < G:
+                load_x("i", g + 1)
+            load_x("cell", g)
+
+        def group_w_gpsimd(k):
+            nc.gpsimd.tensor_scalar(
+                out=walk_out(w_bf[k][:]), in0=walk_in(w_raw[k][:]),
+                scalar1=1.0, scalar2=0.0, op0=ALU.mult, op1=ALU.add,
+            )
+
+        def quantize_w(k):
+            quantize(nc, w_codes[k][:], w_scales[k][:], w_bf[k][:])
+
+        def product(k, bank, g):
+            rows = slice(ROWS * g, ROWS * (g + 1))
+            nc.tensor.matmul_mx(
+                out=bank[g][:],
+                lhsT=w_codes[k][rows, :].bitcast(FP8X4), lhsT_scale=w_scales[k][rows, :],
+                rhs=h_codes[rows, :].bitcast(FP8X4), rhs_scale=h_scales[rows, :],
+                start=True, stop=True,
+            )
+
+        def add_x(pre, bank, k, g):
+            nc.vector.tensor_tensor(out=pre[g][:], in0=bank[g][:], in1=x_sb[k][g][:], op=ALU.add)
+
+        def act(dst, src, func, g, bias=0.0, scale=1.0):
+            nc.scalar.activation(out=dst[g][:], in_=src[g][:], func=func, bias=bias, scale=scale)
+
+        def binary(dst, a, b, op, g, cols=slice(0, N)):
+            nc.vector.tensor_tensor(out=dst[g][:, cols], in0=a[g][:, cols], in1=b[g][:, cols], op=op)
+
+        def v_part(g):
+            nc.vector.scalar_tensor_tensor(
+                out=part_i[g][:], in0=log_k[g][:], scalar=-2.0, in1=bank_b[g][:], op0=ALU.mult, op1=ALU.add
+            )
+
+        def v_pre_a(g):
+            binary(pre_a, part_i, x_sb["i"], ALU.add, g)
+
+        def v_kept(g):
+            nc.vector.scalar_tensor_tensor(
+                out=kept[g][:], in0=beta[g][:], scalar=0.5, in1=x_sb["cell"][g][:], op0=ALU.mult, op1=ALU.mult
+            )
+
+        def v_diff(g, cols=slice(0, N)):
+            binary(diff, cand, kept, ALU.subtract, g, cols)
+
+        def v_step(g, cols=slice(0, N)):
+            binary(step, diff, alpha, ALU.mult, g, cols)
+
+        def v_mixed(g, cols=slice(0, N)):
+            binary(mixed, step, kept, ALU.add, g, cols)
+
+        def v_y(g, cols=slice(0, N)):
+            binary(y, mixed, out_gate, ALU.mult, g, cols)
+
+        def s_beta(g):
+            act(beta, pre_f, ACT.Sigmoid, g, bias=math.log(2.0))
+
+        def s_cand(g):
+            act(cand, pre_c, ACT.Tanh, g)
+
+        def s_alpha(g):
+            act(alpha, pre_a, ACT.Sigmoid, g, scale=0.5)
+
+        def s_out(g):
+            act(out_gate, pre_o, ACT.Sigmoid, g)
+
+        def deal_y(g, quarters):
+            for r in quarters:
+                nc.sync.dma_start(
+                    out=y_dealt[g][ROWS * r : ROWS * (r + 1), :, :],
+                    in_=y[g][:, QUARTER * r : QUARTER * (r + 1)],
+                )
+
+        def store_y(g):
+            nc.sync.dma_start(out=out_0[M * g : M * (g + 1), :], in_=y[g][:])
+
+        def group_y(g):
+            nc.scalar.copy(out=walk_out(y_bf[g][:]), in_=walk_in(y_dealt[g][:]))
+
+        def quantize_y(g):
+            quantize(nc, y_codes[g][:], y_scales[:, g, :], y_bf[g][:])
+
+        words = out_1[0].rearrange("p n t -> p (n t)").bitcast(I32)
+
+        def store_words(g):
+            nc.sync.dma_start(
+                out=words[ROWS * g : ROWS * (g + 1), :].rearrange("q (r n) -> r q n", r=4),
+                in_=y_codes[g][:].bitcast(I32),
+            )
+
+        nc.vector.tensor_copy(out=walk_out(w_bf["f"][:]), in_=walk_in(w_raw["f"][:]))
+        quantize_w("f")
+        for u in range(2):
+            cols = slice(u * HALF, (u + 1) * HALF)
+            nc.vector.tensor_copy(out=walk_out(h_bf[u][:]), in_=walk_in(h_raw[u][:]))
+            quantize(nc, h_codes[:, cols], h_scales[:, cols], h_bf[u][:])
+        for k in ("c", "o", "i"):
+            group_w_gpsimd(k)
+        for g in heads:
+            product("f", bank_a, g)
+        for g in heads:
+            add_x(pre_f, bank_a, "f", g)
+            act(forget, pre_f, ACT.Sigmoid, g)
+            if g == 0:
+                quantize_w("c")
+                for g2 in heads:
+                    product("c", bank_b, g2)
+        for g in range(G - 1):
+            s_beta(g)
+        for g in heads:
+            act(log_k, forget, ACT.Ln, g, bias=1.0)
+        for g in heads:
+            add_x(pre_c, bank_b, "c", g)
+            if g == 0:
+                quantize_w("o")
+                for g2 in heads:
+                    product("o", bank_a, g2)
+        for g in heads:
+            add_x(pre_o, bank_a, "o", g)
+            if g == 1:
+                quantize_w("i")
+                for g2 in heads:
+                    product("i", bank_b, g2)
+
+        v_part(0)
+        v_part(1)
+        v_pre_a(0)
+        v_part(2)
+        v_pre_a(1)
+        v_part(3)
+        v_kept(0)
+        v_pre_a(2)
+        s_cand(0)
+        s_alpha(0)
+        s_out(0)
+        s_cand(1)
+        s_alpha(1)
+        s_beta(3)
+        s_cand(2)
+        s_out(1)
+        s_alpha(2)
+        s_out(2)
+        s_cand(3)
+        v_diff(0)
+        v_kept(1)
+        v_step(0)
+        v_pre_a(3)
+        s_alpha(3)
+        s_out(3)
+        v_mixed(0)
+        v_kept(2)
+        v_y(0)
+        deal_y(0, range(4))
+        store_y(0)
+        group_y(0)
+        v_diff(1)
+        v_kept(3)
+        v_step(1)
+        v_diff(2)
+        v_mixed(1)
+        v_step(2)
+        v_y(1)
+        deal_y(1, range(4))
+        store_y(1)
+        group_y(1)
+        v_mixed(2)
+        quantize_y(0)
+        lo, hi = slice(0, HALF), slice(HALF, N)
+        v_diff(3, lo)
+        v_y(2)
+        deal_y(2, range(4))
+        store_y(2)
+        group_y(2)
+        store_words(0)
+        v_diff(3, hi)
+        for stage in (v_step, v_mixed):
+            stage(3, lo)
+            stage(3, hi)
+        v_y(3, lo)
+        deal_y(3, range(2))
+        v_y(3, hi)
+        deal_y(3, range(2, 4))
+        store_y(3)
+        group_y(3)
+        for g in range(1, G):
+            quantize_y(g)
+            store_words(g)
+        scale_rows = out_2[0].bitcast(I32).rearrange("(g b) (r n) -> r b g n", b=4, r=4)
+        for r in range(4):
+            nc.scalar.dma_start(
+                out=scale_rows[r],
+                in_=y_scales[ROWS * r : ROWS * r + 4, :, :].bitcast(I32),
+            )

@@ -56,8 +56,9 @@ def tile_rows_pl_cell_slstm_kernel(tc, h, wi, wf, wo, wc, xi, xf, xo, xc, c, out
         w_bf = {k: sb.tile([P, M, PACK], BF16, name="w_bf_" + k, align_bytes=64) for k in w_dram}
         w_codes = {k: sb.tile([P, M], U32, name="w_codes_" + k, align_bytes=64) for k in w_dram}
         w_scales = {k: sb.tile([P, M], U8, name="w_scales_" + k, align_bytes=64) for k in w_dram}
+        h_late = [sb.tile([P, QUARTER, PACK], BF16, name="h_late%d" % u, align_bytes=64) for u in range(2)]
         h_raw = [sb.tile([P, PACK, HALF], F32, name="h_raw%d" % u) for u in range(2)]
-        h_bf = [sb.tile([P, HALF, PACK], BF16, name="h_bf%d" % u, align_bytes=64) for u in range(2)]
+        h_early = sb.tile([P, HALF, PACK], BF16, align_bytes=64)
         h_codes = sb.tile([P, N], U32, align_bytes=64)
         h_scales = sb.tile([P, N], U8, align_bytes=64)
 
@@ -83,21 +84,19 @@ def tile_rows_pl_cell_slstm_kernel(tc, h, wi, wf, wo, wc, xi, xf, xo, xc, c, out
         load_w("f")
         for u in range(2):
             nc.sync.dma_start(out=h_raw[u][:], in_=h_rows[:, :, u * HALF : (u + 1) * HALF])
-        for k_w, k_x in (("c", "f"), ("o", "c"), ("i", "o")):
-            load_w(k_w)
+        for k in ("c", "i", "o"):
+            load_w(k)
+        for k in ("f", "c", "cell"):
             for g in heads:
-                load_x(k_x, g)
+                load_x(k, g)
         load_x("i", 0)
         for g in heads:
             if g + 1 < G:
                 load_x("i", g + 1)
-            load_x("cell", g)
+            load_x("o", g)
 
-        def group_w_gpsimd(k):
-            nc.gpsimd.tensor_scalar(
-                out=walk_out(w_bf[k][:]), in0=walk_in(w_raw[k][:]),
-                scalar1=1.0, scalar2=0.0, op0=ALU.mult, op1=ALU.add,
-            )
+        def group_scalar(grouped, raw):
+            nc.scalar.activation(out=walk_out(grouped), in_=walk_in(raw), func=ACT.Copy)
 
         def quantize_w(k):
             quantize(nc, w_codes[k][:], w_scales[k][:], w_bf[k][:])
@@ -122,31 +121,35 @@ def tile_rows_pl_cell_slstm_kernel(tc, h, wi, wf, wo, wc, xi, xf, xo, xc, c, out
 
         def v_part(g):
             nc.vector.scalar_tensor_tensor(
-                out=part_i[g][:], in0=log_k[g][:], scalar=-2.0, in1=bank_b[g][:], op0=ALU.mult, op1=ALU.add
+                out=part_i[g][:], in0=log_k[g][:], scalar=-2.0, in1=bank_a[g][:], op0=ALU.mult, op1=ALU.add
             )
 
-        def v_pre_a(g):
-            binary(pre_a, part_i, x_sb["i"], ALU.add, g)
+        def g_pre_a(g):
+            nc.gpsimd.tensor_tensor(out=pre_a[g][:], in0=part_i[g][:], in1=x_sb["i"][g][:], op=ALU.add)
 
         def v_kept(g):
             nc.vector.scalar_tensor_tensor(
-                out=kept[g][:], in0=beta[g][:], scalar=0.5, in1=x_sb["cell"][g][:], op0=ALU.mult, op1=ALU.mult
+                out=kept[g][:], in0=beta[g][:], scalar=1.0, in1=x_sb["cell"][g][:], op0=ALU.add, op1=ALU.mult
             )
 
         def v_diff(g, cols=slice(0, N)):
-            binary(diff, cand, kept, ALU.subtract, g, cols)
+            nc.vector.scalar_tensor_tensor(
+                out=diff[g][:, cols], in0=kept[g][:, cols], scalar=-0.25, in1=cand[g][:, cols], op0=ALU.mult, op1=ALU.add
+            )
 
         def v_step(g, cols=slice(0, N)):
             binary(step, diff, alpha, ALU.mult, g, cols)
 
         def v_mixed(g, cols=slice(0, N)):
-            binary(mixed, step, kept, ALU.add, g, cols)
+            nc.vector.scalar_tensor_tensor(
+                out=mixed[g][:, cols], in0=kept[g][:, cols], scalar=0.25, in1=step[g][:, cols], op0=ALU.mult, op1=ALU.add
+            )
 
         def v_y(g, cols=slice(0, N)):
             binary(y, mixed, out_gate, ALU.mult, g, cols)
 
         def s_beta(g):
-            act(beta, pre_f, ACT.Sigmoid, g, bias=math.log(2.0))
+            act(beta, pre_f, ACT.Tanh, g, bias=0.5 * math.log(2.0), scale=0.5)
 
         def s_cand(g):
             act(cand, pre_c, ACT.Tanh, g)
@@ -168,7 +171,7 @@ def tile_rows_pl_cell_slstm_kernel(tc, h, wi, wf, wo, wc, xi, xf, xo, xc, c, out
             nc.sync.dma_start(out=out_0[M * g : M * (g + 1), :], in_=y[g][:])
 
         def group_y(g):
-            nc.scalar.copy(out=walk_out(y_bf[g][:]), in_=walk_in(y_dealt[g][:]))
+            group_scalar(y_bf[g][:], y_dealt[g][:])
 
         def quantize_y(g):
             quantize(nc, y_codes[g][:], y_scales[:, g, :], y_bf[g][:])
@@ -181,106 +184,85 @@ def tile_rows_pl_cell_slstm_kernel(tc, h, wi, wf, wo, wc, xi, xf, xo, xc, c, out
                 in_=y_codes[g][:].bitcast(I32),
             )
 
-        nc.vector.tensor_copy(out=walk_out(w_bf["f"][:]), in_=walk_in(w_raw["f"][:]))
+        group_scalar(w_bf["f"][:], w_raw["f"][:])
         quantize_w("f")
+        nc.vector.tensor_copy(out=walk_out(h_early[:]), in_=walk_in(h_raw[0][:]))
+        quantize(nc, h_codes[:, 0:HALF], h_scales[:, 0:HALF], h_early[:])
+        nc.vector.tensor_copy(out=walk_out(h_late[0][:]), in_=walk_in(h_raw[1][:, :, 0:QUARTER]))
+        group_scalar(h_late[1][:], h_raw[1][:, :, QUARTER:HALF])
         for u in range(2):
-            cols = slice(u * HALF, (u + 1) * HALF)
-            nc.vector.tensor_copy(out=walk_out(h_bf[u][:]), in_=walk_in(h_raw[u][:]))
-            quantize(nc, h_codes[:, cols], h_scales[:, cols], h_bf[u][:])
-        for k in ("c", "o", "i"):
-            group_w_gpsimd(k)
+            cols = slice(HALF + u * QUARTER, HALF + (u + 1) * QUARTER)
+            quantize(nc, h_codes[:, cols], h_scales[:, cols], h_late[u][:])
+        for k in ("c", "i", "o"):
+            group_scalar(w_bf[k][:], w_raw[k][:])
         for g in heads:
             product("f", bank_a, g)
+        quantize_w("c")
+        for g in heads:
+            product("c", bank_b, g)
         for g in heads:
             add_x(pre_f, bank_a, "f", g)
-            act(forget, pre_f, ACT.Sigmoid, g)
-            if g == 0:
-                quantize_w("c")
-                for g2 in heads:
-                    product("c", bank_b, g2)
-        for g in range(G - 1):
+            act(forget, pre_f, ACT.Tanh, g, scale=0.5)
             s_beta(g)
-        for g in heads:
-            act(log_k, forget, ACT.Ln, g, bias=1.0)
-        for g in heads:
-            add_x(pre_c, bank_b, "c", g)
-            if g == 0:
-                quantize_w("o")
-                for g2 in heads:
-                    product("o", bank_a, g2)
-        for g in heads:
-            add_x(pre_o, bank_a, "o", g)
             if g == 1:
                 quantize_w("i")
-                for g2 in heads:
-                    product("i", bank_b, g2)
-
+                quantize_w("o")
+        for g in heads:
+            product("i", bank_a, g)
+        for g in heads:
+            act(log_k, forget, ACT.Ln, g, bias=1.5, scale=0.5)
+        for g in heads:
+            add_x(pre_c, bank_b, "c", g)
+        for g in heads:
+            product("o", bank_b, g)
+        for g in heads:
+            v_kept(g)
         v_part(0)
-        v_part(1)
-        v_pre_a(0)
-        v_part(2)
-        v_pre_a(1)
-        v_part(3)
-        v_kept(0)
-        v_pre_a(2)
-        s_cand(0)
+        g_pre_a(0)
+        for g in heads:
+            if g + 1 < G:
+                v_part(g + 1)
+                g_pre_a(g + 1)
+            add_x(pre_o, bank_b, "o", g)
+
         s_alpha(0)
-        s_out(0)
+        s_cand(0)
         s_cand(1)
+        s_out(0)
         s_alpha(1)
-        s_beta(3)
         s_cand(2)
         s_out(1)
         s_alpha(2)
         s_out(2)
         s_cand(3)
-        v_diff(0)
-        v_kept(1)
-        v_step(0)
-        v_pre_a(3)
         s_alpha(3)
         s_out(3)
-        v_mixed(0)
-        v_kept(2)
-        v_y(0)
-        deal_y(0, range(4))
-        store_y(0)
-        group_y(0)
-        v_diff(1)
-        v_kept(3)
-        v_step(1)
-        v_diff(2)
-        v_mixed(1)
-        v_step(2)
-        v_y(1)
-        deal_y(1, range(4))
-        store_y(1)
-        group_y(1)
-        v_mixed(2)
-        quantize_y(0)
+        for stage in (v_diff, v_step, v_mixed):
+            stage(0)
+            stage(1)
         lo, hi = slice(0, HALF), slice(HALF, N)
+        v_y(0)
+        v_diff(2)
+        v_y(1)
+        v_step(2)
         v_diff(3, lo)
-        v_y(2)
-        deal_y(2, range(4))
-        store_y(2)
-        group_y(2)
-        store_words(0)
+        v_mixed(2)
         v_diff(3, hi)
-        for stage in (v_step, v_mixed):
+        v_y(2)
+        for stage in (v_step, v_mixed, v_y):
             stage(3, lo)
             stage(3, hi)
-        v_y(3, lo)
-        deal_y(3, range(2))
-        v_y(3, hi)
-        deal_y(3, range(2, 4))
-        store_y(3)
-        group_y(3)
-        for g in range(1, G):
+        for g in heads:
+            deal_y(g, range(4))
+            store_y(g)
+            group_y(g)
+        for g in heads:
             quantize_y(g)
             store_words(g)
         scale_rows = out_2[0].bitcast(I32).rearrange("(g b) (r n) -> r b g n", b=4, r=4)
         for r in range(4):
-            nc.scalar.dma_start(
+            queue = nc.sync if r == 3 else nc.scalar
+            queue.dma_start(
                 out=scale_rows[r],
                 in_=y_scales[ROWS * r : ROWS * r + 4, :, :].bitcast(I32),
             )

@@ -21,6 +21,8 @@ ROWS = 32
 RUN = 4
 HALF = N // 2
 QUARTER = N // 4
+LAST = G - 1
+EIGHTH = QUARTER // 2
 
 
 def walk_in(raw):
@@ -63,13 +65,17 @@ def tile_rows_pl_cell_slstm_kernel(tc, h, wi, wf, wo, wc, xi, xf, xo, xc, c, out
         h_scales = sb.tile([P, N], U8, align_bytes=64)
 
         x_dram = {"f": xf, "c": xc, "o": xo, "i": xi, "cell": c}
-        x_sb = {k: per_head("x_" + k) for k in x_dram}
+        x_pair = {k: [sb.tile([P, 2, N], F32, name="x_%s%d" % (k, u)) for u in range(2)] for k in x_dram}
+        x_sb = {k: [x_pair[k][g // 2][:, g % 2, :] for g in heads] for k in x_dram}
         pre_f, pre_c, pre_o = per_head("pre_f"), per_head("pre_c"), per_head("pre_o")
         forget, log_k, beta = per_head("forget"), per_head("log_k"), per_head("beta")
         cand, out_gate = per_head("cand"), per_head("out_gate")
         part_i, pre_a, alpha = per_head("part_i"), per_head("pre_a"), per_head("alpha")
         kept, diff, step, mixed, y = (per_head(n) for n in ("kept", "diff", "step", "mixed", "y"))
-        y_dealt = [sb.tile([P, PACK, QUARTER], F32, name="y_dealt%d" % g) for g in heads]
+        y_dealt = [sb.tile([P, N], F32, name="y_dealt%d" % g) for g in range(LAST)] + [y[LAST]]
+        early = {n: sb.tile([P, N], F32, name="early_" + n) for n in ("pre_c", "pre_o", "pre_a", "kept")}
+        pre_c_in, pre_o_in = pre_c[:LAST] + [early["pre_c"]], pre_o[:LAST] + [early["pre_o"]]
+        pre_a_in, kept_in = pre_a[:LAST] + [early["pre_a"]], kept[:LAST] + [early["kept"]]
         y_bf = [sb.tile([P, QUARTER, PACK], BF16, name="y_bf%d" % g, align_bytes=64) for g in heads]
         y_codes = [sb.tile([P, QUARTER], U32, name="y_codes%d" % g, align_bytes=64) for g in heads]
         y_scales = sb.tile([P, G, QUARTER], U8, align_bytes=64)
@@ -77,23 +83,30 @@ def tile_rows_pl_cell_slstm_kernel(tc, h, wi, wf, wo, wc, xi, xf, xo, xc, c, out
         def load_w(k):
             nc.sync.dma_start(out=w_raw[k][:], in_=w_dram[k].rearrange("g (p t) m -> (g p) t m", t=PACK))
 
-        def load_x(k, g):
-            nc.sync.dma_start(out=x_sb[k][g][:], in_=x_dram[k][g])
+        def load_x(k, u):
+            nc.sync.dma_start(out=x_pair[k][u][:], in_=x_dram[k][2 * u : 2 * u + 2].rearrange("g m n -> m g n"))
 
         h_rows = h.rearrange("g (p t) n -> (g p) t n", t=PACK)
         load_w("f")
         for u in range(2):
             nc.sync.dma_start(out=h_raw[u][:], in_=h_rows[:, :, u * HALF : (u + 1) * HALF])
-        for k in ("c", "i", "o"):
-            load_w(k)
-        for k in ("f", "c", "cell"):
-            for g in heads:
-                load_x(k, g)
-        load_x("i", 0)
-        for g in heads:
-            if g + 1 < G:
-                load_x("i", g + 1)
-            load_x("o", g)
+        load_x("f", 0)
+        load_w("c")
+        load_x("f", 1)
+        load_w("i")
+        load_w("o")
+        for k in ("c", "cell"):
+            for u in range(2):
+                load_x(k, u)
+        for u in range(2):
+            load_x("i", u)
+            load_x("o", u)
+
+        def group_gpsimd(k):
+            nc.gpsimd.tensor_scalar(
+                out=w_bf[k][:], in0=w_raw[k][:].rearrange("p t m -> p m t"),
+                scalar1=1.0, scalar2=0.0, op0=ALU.mult, op1=ALU.add,
+            )
 
         def group_scalar(grouped, raw):
             nc.scalar.activation(out=walk_out(grouped), in_=walk_in(raw), func=ACT.Copy)
@@ -111,13 +124,23 @@ def tile_rows_pl_cell_slstm_kernel(tc, h, wi, wf, wo, wc, xi, xf, xo, xc, c, out
             )
 
         def add_x(pre, bank, k, g):
-            nc.vector.tensor_tensor(out=pre[g][:], in0=bank[g][:], in1=x_sb[k][g][:], op=ALU.add)
+            nc.vector.tensor_tensor(out=pre[g][:], in0=bank[g][:], in1=x_sb[k][g], op=ALU.add)
 
         def act(dst, src, func, g, bias=0.0, scale=1.0):
             nc.scalar.activation(out=dst[g][:], in_=src[g][:], func=func, bias=bias, scale=scale)
 
-        def binary(dst, a, b, op, g, cols=slice(0, N)):
-            nc.vector.tensor_tensor(out=dst[g][:, cols], in0=a[g][:, cols], in1=b[g][:, cols], op=op)
+        def part(tile, u):
+            if u is None:
+                return tile[:]
+            return tile[:].rearrange("p (t n) -> p t n", t=PACK)[:, :, u * EIGHTH : (u + 1) * EIGHTH]
+
+        def binary(dst, a, b, op, g, u):
+            nc.vector.tensor_tensor(out=part(dst[g], u), in0=part(a[g], u), in1=part(b[g], u), op=op)
+
+        def scaled_add(dst, factor, b, g, u):
+            nc.vector.scalar_tensor_tensor(
+                out=part(dst[g], u), in0=part(kept_in[g], u), scalar=factor, in1=part(b[g], u), op0=ALU.mult, op1=ALU.add
+            )
 
         def v_part(g):
             nc.vector.scalar_tensor_tensor(
@@ -125,53 +148,56 @@ def tile_rows_pl_cell_slstm_kernel(tc, h, wi, wf, wo, wc, xi, xf, xo, xc, c, out
             )
 
         def g_pre_a(g):
-            nc.gpsimd.tensor_tensor(out=pre_a[g][:], in0=part_i[g][:], in1=x_sb["i"][g][:], op=ALU.add)
+            nc.gpsimd.tensor_tensor(out=pre_a[g][:], in0=part_i[g][:], in1=x_sb["i"][g], op=ALU.add)
 
         def v_kept(g):
             nc.vector.scalar_tensor_tensor(
-                out=kept[g][:], in0=beta[g][:], scalar=1.0, in1=x_sb["cell"][g][:], op0=ALU.add, op1=ALU.mult
+                out=kept[g][:], in0=beta[g][:], scalar=1.0, in1=x_sb["cell"][g], op0=ALU.add, op1=ALU.mult
             )
 
-        def v_diff(g, cols=slice(0, N)):
-            nc.vector.scalar_tensor_tensor(
-                out=diff[g][:, cols], in0=kept[g][:, cols], scalar=-0.25, in1=cand[g][:, cols], op0=ALU.mult, op1=ALU.add
-            )
+        def v_diff(g, u=None):
+            scaled_add(diff, -0.25, cand, g, u)
 
-        def v_step(g, cols=slice(0, N)):
-            binary(step, diff, alpha, ALU.mult, g, cols)
+        def v_step(g, u=None):
+            binary(step, diff, alpha, ALU.mult, g, u)
 
-        def v_mixed(g, cols=slice(0, N)):
-            nc.vector.scalar_tensor_tensor(
-                out=mixed[g][:, cols], in0=kept[g][:, cols], scalar=0.25, in1=step[g][:, cols], op0=ALU.mult, op1=ALU.add
-            )
+        def v_mixed(g, u=None):
+            scaled_add(mixed, 0.25, step, g, u)
 
-        def v_y(g, cols=slice(0, N)):
-            binary(y, mixed, out_gate, ALU.mult, g, cols)
+        def v_y(g, u=None):
+            binary(y, mixed, out_gate, ALU.mult, g, u)
 
         def s_beta(g):
             act(beta, pre_f, ACT.Tanh, g, bias=0.5 * math.log(2.0), scale=0.5)
 
         def s_cand(g):
-            act(cand, pre_c, ACT.Tanh, g)
+            act(cand, pre_c_in, ACT.Tanh, g)
 
         def s_alpha(g):
-            act(alpha, pre_a, ACT.Sigmoid, g, scale=0.5)
+            act(alpha, pre_a_in, ACT.Sigmoid, g, scale=0.5)
 
         def s_out(g):
-            act(out_gate, pre_o, ACT.Sigmoid, g)
+            act(out_gate, pre_o_in, ACT.Sigmoid, g)
 
-        def deal_y(g, quarters):
-            for r in quarters:
+        def deal(dst, src):
+            for r in range(4):
                 nc.sync.dma_start(
-                    out=y_dealt[g][ROWS * r : ROWS * (r + 1), :, :],
-                    in_=y[g][:, QUARTER * r : QUARTER * (r + 1)],
+                    out=dst[ROWS * r : ROWS * (r + 1), :].rearrange("q (t n) -> q t n", t=PACK),
+                    in_=src[:, QUARTER * r : QUARTER * (r + 1)],
                 )
 
         def store_y(g):
             nc.sync.dma_start(out=out_0[M * g : M * (g + 1), :], in_=y[g][:])
 
+        def store_dealt_y(g):
+            rows = out_0[M * g : M * (g + 1), :].rearrange("(q t) (r n) -> r q t n", t=PACK, r=4)
+            for r in range(4):
+                nc.sync.dma_start(
+                    out=rows[r], in_=y[g][ROWS * r : ROWS * (r + 1), :].rearrange("q (t n) -> q t n", t=PACK)
+                )
+
         def group_y(g):
-            group_scalar(y_bf[g][:], y_dealt[g][:])
+            group_scalar(y_bf[g][:], y_dealt[g][:].rearrange("p (t n) -> p t n", t=PACK))
 
         def quantize_y(g):
             quantize(nc, y_codes[g][:], y_scales[:, g, :], y_bf[g][:])
@@ -193,76 +219,103 @@ def tile_rows_pl_cell_slstm_kernel(tc, h, wi, wf, wo, wc, xi, xf, xo, xc, c, out
         for u in range(2):
             cols = slice(HALF + u * QUARTER, HALF + (u + 1) * QUARTER)
             quantize(nc, h_codes[:, cols], h_scales[:, cols], h_late[u][:])
-        for k in ("c", "i", "o"):
-            group_scalar(w_bf[k][:], w_raw[k][:])
+        group_scalar(w_bf["c"][:], w_raw["c"][:])
+        group_gpsimd("i")
+        group_gpsimd("o")
         for g in heads:
             product("f", bank_a, g)
-        quantize_w("c")
-        for g in heads:
-            product("c", bank_b, g)
         for g in heads:
             add_x(pre_f, bank_a, "f", g)
             act(forget, pre_f, ACT.Tanh, g, scale=0.5)
             s_beta(g)
-            if g == 1:
-                quantize_w("i")
-                quantize_w("o")
+            if g == 0:
+                quantize_w("c")
         for g in heads:
-            product("i", bank_a, g)
+            product("c", bank_b, g)
         for g in heads:
             act(log_k, forget, ACT.Ln, g, bias=1.5, scale=0.5)
         for g in heads:
             add_x(pre_c, bank_b, "c", g)
+        quantize_w("i")
+        quantize_w("o")
+        for g in heads:
+            product("i", bank_a, g)
         for g in heads:
             product("o", bank_b, g)
         for g in heads:
             v_kept(g)
+        deal(early["pre_c"], pre_c[LAST])
+        deal(early["kept"], kept[LAST])
         v_part(0)
         g_pre_a(0)
         for g in heads:
             if g + 1 < G:
                 v_part(g + 1)
+            if g + 1 < LAST:
                 g_pre_a(g + 1)
             add_x(pre_o, bank_b, "o", g)
+        nc.vector.tensor_tensor(out=pre_a[LAST][:], in0=part_i[LAST][:], in1=x_sb["i"][LAST], op=ALU.add)
+        deal(early["pre_o"], pre_o[LAST])
+        deal(early["pre_a"], pre_a[LAST])
 
         s_alpha(0)
         s_cand(0)
         s_cand(1)
-        s_out(0)
         s_alpha(1)
         s_cand(2)
-        s_out(1)
+        s_out(0)
         s_alpha(2)
+        s_out(1)
         s_out(2)
         s_cand(3)
         s_alpha(3)
         s_out(3)
-        for stage in (v_diff, v_step, v_mixed):
-            stage(0)
-            stage(1)
-        lo, hi = slice(0, HALF), slice(HALF, N)
-        v_y(0)
+
+        v_diff(0)
+        v_diff(1)
+        v_step(0)
+        v_step(1)
+        v_mixed(0)
         v_diff(2)
-        v_y(1)
+        v_y(0)
+        deal(y_dealt[0], y[0])
+        store_y(0)
+        group_y(0)
+        v_mixed(1)
         v_step(2)
-        v_diff(3, lo)
+        v_y(1)
+        deal(y_dealt[1], y[1])
+        group_y(1)
         v_mixed(2)
-        v_diff(3, hi)
+        v_diff(3, 0)
         v_y(2)
-        for stage in (v_step, v_mixed, v_y):
-            stage(3, lo)
-            stage(3, hi)
-        for g in heads:
-            deal_y(g, range(4))
-            store_y(g)
-            group_y(g)
-        for g in heads:
-            quantize_y(g)
-            store_words(g)
+        deal(y_dealt[2], y[2])
+        store_y(1)
+        store_y(2)
+        group_y(2)
+        v_diff(3, 1)
+        v_step(3, 0)
+        v_step(3, 1)
+        quantize_y(0)
+        store_words(0)
+        v_mixed(3, 0)
+        v_mixed(3, 1)
+        v_y(3, 0)
+        v_y(3, 1)
+        store_dealt_y(3)
+        for u in range(2):
+            nc.vector.tensor_copy(
+                out=walk_out(y_bf[3][:, u * EIGHTH : (u + 1) * EIGHTH, :]), in_=walk_in(part(y[3], u))
+            )
+        quantize_y(1)
+        store_words(1)
+        quantize_y(3)
+        store_words(3)
+        quantize_y(2)
+        store_words(2)
         scale_rows = out_2[0].bitcast(I32).rearrange("(g b) (r n) -> r b g n", b=4, r=4)
         for r in range(4):
-            queue = nc.sync if r == 3 else nc.scalar
-            queue.dma_start(
+            nc.scalar.dma_start(
                 out=scale_rows[r],
                 in_=y_scales[ROWS * r : ROWS * r + 4, :, :].bitcast(I32),
             )

@@ -17,26 +17,36 @@ ACT = mybir.ActivationFunctionType
 
 P = 128
 PACK = 4
-ROWS = 32
+ROWS = D // PACK
+SCALE_ROWS = 4
 RUN = 4
 HALF = N // 2
 QUARTER = N // 4
-LAST = G - 1
-EIGHTH = QUARTER // 2
-
-
-def walk_in(raw):
-    return raw.rearrange("p t (c i) -> p c t i", i=RUN)
-
-
-def walk_out(grouped):
-    return grouped.rearrange("p (c i) t -> p c t i", i=RUN)
+LATE_HEADS = (0, 1)
+EARLY_HEADS = (2, 3)
 
 
 def quantize(nc, codes, scales, grouped):
     nc.vector.quantize_mx(
         out=codes.bitcast(FP8X4), scales=scales, in_=grouped.rearrange("p c t -> p (c t)")
     )
+
+
+def regroup_views(grouped, raw):
+    return (
+        grouped.rearrange("p (c i) t -> p c t i", i=RUN),
+        raw.rearrange("p t (c i) -> p c t i", i=RUN),
+    )
+
+
+def regroup_on_scalar(nc, grouped, raw):
+    out, in_ = regroup_views(grouped, raw)
+    nc.scalar.activation(out=out, in_=in_, func=ACT.Copy)
+
+
+def regroup_on_vector(nc, grouped, raw):
+    out, in_ = regroup_views(grouped, raw)
+    nc.vector.tensor_copy(out=out, in_=in_)
 
 
 def tile_rows_pl_cell_slstm_kernel(tc, h, wi, wf, wo, wc, xi, xf, xo, xc, c, out_0, out_1, out_2):
@@ -47,275 +57,196 @@ def tile_rows_pl_cell_slstm_kernel(tc, h, wi, wf, wo, wc, xi, xf, xo, xc, c, out
         psum = ctx.enter_context(tc.psum_pool(name="psum", bufs=1))
         ctx.enter_context(tc.manual_schedule())
 
-        def per_head(name):
-            return [sb.tile([P, N], F32, name="%s%d" % (name, g)) for g in heads]
+        def natural_tiles(name, which):
+            return {g: sb.tile([P, N], F32, name="%s%d" % (name, g))[:] for g in which}
 
-        bank_a = [psum.tile([M, N], F32, name="bank_a%d" % g) for g in heads]
-        bank_b = [psum.tile([M, N], F32, name="bank_b%d" % g) for g in heads]
+        def dealt_tile(name):
+            return sb.tile([P, PACK, HALF], F32, name=name)[:]
 
-        w_dram = {"f": wf, "c": wc, "o": wo, "i": wi}
-        w_raw = {k: sb.tile([P, PACK, M], F32, name="w_raw_" + k) for k in w_dram}
-        w_bf = {k: sb.tile([P, M, PACK], BF16, name="w_bf_" + k, align_bytes=64) for k in w_dram}
-        w_codes = {k: sb.tile([P, M], U32, name="w_codes_" + k, align_bytes=64) for k in w_dram}
-        w_scales = {k: sb.tile([P, M], U8, name="w_scales_" + k, align_bytes=64) for k in w_dram}
-        h_late = [sb.tile([P, QUARTER, PACK], BF16, name="h_late%d" % u, align_bytes=64) for u in range(2)]
-        h_raw = [sb.tile([P, PACK, HALF], F32, name="h_raw%d" % u) for u in range(2)]
-        h_early = sb.tile([P, HALF, PACK], BF16, align_bytes=64)
-        h_codes = sb.tile([P, N], U32, align_bytes=64)
-        h_scales = sb.tile([P, N], U8, align_bytes=64)
+        def column_halves(dealt):
+            return [dealt[:, :, 0:QUARTER], dealt[:, :, QUARTER:HALF]]
 
-        x_dram = {"f": xf, "c": xc, "o": xo, "i": xi, "cell": c}
-        x_pair = {k: [sb.tile([P, 2, N], F32, name="x_%s%d" % (k, u)) for u in range(2)] for k in x_dram}
+        bank_a = [psum.tile([M, N], F32, name="bank_a%d" % g)[:] for g in heads]
+        bank_b = [psum.tile([M, N], F32, name="bank_b%d" % g)[:] for g in heads]
+
+        w_dram = {"f": wf, "c": wc, "i": wi, "o": wo}
+        w_raw = {k: sb.tile([P, PACK, M], F32, name="w_raw_" + k)[:] for k in w_dram}
+        w_bf = {k: sb.tile([P, M, PACK], BF16, name="w_bf_" + k, align_bytes=64)[:] for k in w_dram}
+        w_codes = {k: sb.tile([P, M], U32, name="w_codes_" + k, align_bytes=64)[:] for k in w_dram}
+        w_scales = {k: sb.tile([P, M], U8, name="w_scales_" + k, align_bytes=64)[:] for k in w_dram}
+        h_raw = [sb.tile([P, PACK, HALF], F32, name="h_raw%d" % half)[:] for half in range(2)]
+        h_bf_first = sb.tile([P, HALF, PACK], BF16, name="h_bf_first", align_bytes=64)[:]
+        h_bf_last = [sb.tile([P, QUARTER, PACK], BF16, name="h_bf_last%d" % part, align_bytes=64)[:] for part in range(2)]
+        h_codes = sb.tile([P, N], U32, name="h_codes", align_bytes=64)[:]
+        h_scales = sb.tile([P, N], U8, name="h_scales", align_bytes=64)[:]
+
+        x_dram = {"f": xf, "c": xc, "i": xi, "o": xo, "cell": c}
+        x_pair = {k: [sb.tile([P, 2, N], F32, name="x_%s%d" % (k, pair))[:] for pair in range(2)] for k in x_dram}
         x_sb = {k: [x_pair[k][g // 2][:, g % 2, :] for g in heads] for k in x_dram}
-        pre_f, pre_c, pre_o = per_head("pre_f"), per_head("pre_c"), per_head("pre_o")
-        forget, log_k, beta = per_head("forget"), per_head("log_k"), per_head("beta")
-        cand, out_gate = per_head("cand"), per_head("out_gate")
-        part_i, pre_a, alpha = per_head("part_i"), per_head("pre_a"), per_head("alpha")
-        kept, diff, step, mixed, y = (per_head(n) for n in ("kept", "diff", "step", "mixed", "y"))
-        y_dealt = [sb.tile([P, N], F32, name="y_dealt%d" % g) for g in range(LAST)] + [y[LAST]]
-        early = {n: sb.tile([P, N], F32, name="early_" + n) for n in ("pre_c", "pre_o", "pre_a", "kept")}
-        pre_c_in, pre_o_in = pre_c[:LAST] + [early["pre_c"]], pre_o[:LAST] + [early["pre_o"]]
-        pre_a_in, kept_in = pre_a[:LAST] + [early["pre_a"]], kept[:LAST] + [early["kept"]]
-        y_bf = [sb.tile([P, QUARTER, PACK], BF16, name="y_bf%d" % g, align_bytes=64) for g in heads]
-        y_codes = [sb.tile([P, QUARTER], U32, name="y_codes%d" % g, align_bytes=64) for g in heads]
-        y_scales = sb.tile([P, G, QUARTER], U8, align_bytes=64)
+
+        a_f, a_c, a_o = (natural_tiles(name, heads) for name in ("a_f", "a_c", "a_o"))
+        tanh_f, tanh_shifted, log_1s = (natural_tiles(name, heads) for name in ("tanh_f", "tanh_shifted", "log_1s"))
+        z_less_log, a_alpha, alpha = (natural_tiles(name, heads) for name in ("z_less_log", "a_alpha", "alpha"))
+        kept, cand, diff, step = (natural_tiles(name, heads) for name in ("kept", "cand", "diff", "step"))
+        gate_o, mixed, y = (natural_tiles(name, EARLY_HEADS) for name in ("gate_o", "mixed", "y"))
+        kept_late, a_o_late, step_late = (dealt_tile(name) for name in ("kept_late", "a_o_late", "step_late"))
+        gate_o_late, mixed_late, y_late = (dealt_tile(name) for name in ("gate_o_late", "mixed_late", "y_late"))
+        y_early = dealt_tile("y_early")
+        y_bf = [sb.tile([P, HALF, PACK], BF16, name="y_bf%d" % pair, align_bytes=64)[:] for pair in range(2)]
+        y_codes = sb.tile([P, 2, HALF], U32, name="y_codes", align_bytes=64)[:]
+        y_scales = sb.tile([P, 2, HALF], U8, name="y_scales", align_bytes=64)[:]
 
         def load_w(k):
-            nc.sync.dma_start(out=w_raw[k][:], in_=w_dram[k].rearrange("g (p t) m -> (g p) t m", t=PACK))
+            nc.sync.dma_start(out=w_raw[k], in_=w_dram[k].rearrange("g (p t) m -> (g p) t m", t=PACK))
 
-        def load_x(k, u):
-            nc.sync.dma_start(out=x_pair[k][u][:], in_=x_dram[k][2 * u : 2 * u + 2].rearrange("g m n -> m g n"))
+        def load_x(k, pair):
+            nc.sync.dma_start(out=x_pair[k][pair], in_=x_dram[k][2 * pair : 2 * pair + 2].rearrange("g m n -> m g n"))
+
+        def quantize_w(k):
+            quantize(nc, w_codes[k], w_scales[k], w_bf[k])
+
+        def products(k, bank):
+            for g in heads:
+                rows = slice(ROWS * g, ROWS * (g + 1))
+                nc.tensor.matmul_mx(
+                    out=bank[g],
+                    lhsT=w_codes[k][rows, :].bitcast(FP8X4),
+                    lhsT_scale=w_scales[k][rows, :],
+                    rhs=h_codes[rows, :].bitcast(FP8X4),
+                    rhs_scale=h_scales[rows, :],
+                    start=True,
+                    stop=True,
+                )
+
+        def act(out, in_, func, bias=0.0, scale=1.0):
+            nc.scalar.activation(out=out, in_=in_, func=func, bias=bias, scale=scale)
+
+        def add(engine, out, a, b):
+            engine.tensor_tensor(out=out, in0=a, in1=b, op=ALU.add)
+
+        def multiply(out, a, b):
+            nc.vector.tensor_tensor(out=out, in0=a, in1=b, op=ALU.mult)
+
+        def scaled_add(out, a, factor, b):
+            nc.vector.scalar_tensor_tensor(out=out, in0=a, scalar=factor, in1=b, op0=ALU.mult, op1=ALU.add)
+
+        def deal(dealt, natural, pair_heads, queues):
+            for g in pair_heads:
+                for half, queue in enumerate(queues):
+                    first = 2 * ROWS * half + ROWS * (g % 2)
+                    queue.dma_start(
+                        out=dealt[first : first + ROWS, :, :], in_=natural[g][:, HALF * half : HALF * (half + 1)]
+                    )
+
+        sync_only, both_queues = (nc.sync, nc.sync), (nc.sync, nc.scalar)
 
         h_rows = h.rearrange("g (p t) n -> (g p) t n", t=PACK)
         load_w("f")
-        for u in range(2):
-            nc.sync.dma_start(out=h_raw[u][:], in_=h_rows[:, :, u * HALF : (u + 1) * HALF])
+        for half in range(2):
+            nc.sync.dma_start(out=h_raw[half], in_=h_rows[:, :, half * HALF : (half + 1) * HALF])
         load_x("f", 0)
         load_w("c")
-        load_x("f", 1)
         load_w("i")
+        load_x("f", 1)
         load_w("o")
         for k in ("c", "cell"):
-            for u in range(2):
-                load_x(k, u)
-        for u in range(2):
-            load_x("i", u)
-            load_x("o", u)
+            for pair in range(2):
+                load_x(k, pair)
+        for pair in range(2):
+            load_x("i", pair)
+            load_x("o", pair)
 
-        def group_gpsimd(k):
-            nc.gpsimd.tensor_scalar(
-                out=w_bf[k][:], in0=w_raw[k][:].rearrange("p t m -> p m t"),
-                scalar1=1.0, scalar2=0.0, op0=ALU.mult, op1=ALU.add,
-            )
-
-        def group_scalar(grouped, raw):
-            nc.scalar.activation(out=walk_out(grouped), in_=walk_in(raw), func=ACT.Copy)
-
-        def quantize_w(k):
-            quantize(nc, w_codes[k][:], w_scales[k][:], w_bf[k][:])
-
-        def product(k, bank, g):
-            rows = slice(ROWS * g, ROWS * (g + 1))
-            nc.tensor.matmul_mx(
-                out=bank[g][:],
-                lhsT=w_codes[k][rows, :].bitcast(FP8X4), lhsT_scale=w_scales[k][rows, :],
-                rhs=h_codes[rows, :].bitcast(FP8X4), rhs_scale=h_scales[rows, :],
-                start=True, stop=True,
-            )
-
-        def add_x(pre, bank, k, g):
-            nc.vector.tensor_tensor(out=pre[g][:], in0=bank[g][:], in1=x_sb[k][g], op=ALU.add)
-
-        def act(dst, src, func, g, bias=0.0, scale=1.0):
-            nc.scalar.activation(out=dst[g][:], in_=src[g][:], func=func, bias=bias, scale=scale)
-
-        def part(tile, u):
-            if u is None:
-                return tile[:]
-            return tile[:].rearrange("p (t n) -> p t n", t=PACK)[:, :, u * EIGHTH : (u + 1) * EIGHTH]
-
-        def binary(dst, a, b, op, g, u):
-            nc.vector.tensor_tensor(out=part(dst[g], u), in0=part(a[g], u), in1=part(b[g], u), op=op)
-
-        def scaled_add(dst, factor, b, g, u):
-            nc.vector.scalar_tensor_tensor(
-                out=part(dst[g], u), in0=part(kept_in[g], u), scalar=factor, in1=part(b[g], u), op0=ALU.mult, op1=ALU.add
-            )
-
-        def v_part(g):
-            nc.vector.scalar_tensor_tensor(
-                out=part_i[g][:], in0=log_k[g][:], scalar=-2.0, in1=bank_a[g][:], op0=ALU.mult, op1=ALU.add
-            )
-
-        def g_pre_a(g):
-            nc.gpsimd.tensor_tensor(out=pre_a[g][:], in0=part_i[g][:], in1=x_sb["i"][g], op=ALU.add)
-
-        def v_kept(g):
-            nc.vector.scalar_tensor_tensor(
-                out=kept[g][:], in0=beta[g][:], scalar=1.0, in1=x_sb["cell"][g], op0=ALU.add, op1=ALU.mult
-            )
-
-        def v_diff(g, u=None):
-            scaled_add(diff, -0.25, cand, g, u)
-
-        def v_step(g, u=None):
-            binary(step, diff, alpha, ALU.mult, g, u)
-
-        def v_mixed(g, u=None):
-            scaled_add(mixed, 0.25, step, g, u)
-
-        def v_y(g, u=None):
-            binary(y, mixed, out_gate, ALU.mult, g, u)
-
-        def s_beta(g):
-            act(beta, pre_f, ACT.Tanh, g, bias=0.5 * math.log(2.0), scale=0.5)
-
-        def s_cand(g):
-            act(cand, pre_c_in, ACT.Tanh, g)
-
-        def s_alpha(g):
-            act(alpha, pre_a_in, ACT.Sigmoid, g, scale=0.5)
-
-        def s_out(g):
-            act(out_gate, pre_o_in, ACT.Sigmoid, g)
-
-        def deal(dst, src):
-            for r in range(4):
-                nc.sync.dma_start(
-                    out=dst[ROWS * r : ROWS * (r + 1), :].rearrange("q (t n) -> q t n", t=PACK),
-                    in_=src[:, QUARTER * r : QUARTER * (r + 1)],
-                )
-
-        def store_y(g):
-            nc.sync.dma_start(out=out_0[M * g : M * (g + 1), :], in_=y[g][:])
-
-        def store_dealt_y(g):
-            rows = out_0[M * g : M * (g + 1), :].rearrange("(q t) (r n) -> r q t n", t=PACK, r=4)
-            for r in range(4):
-                nc.sync.dma_start(
-                    out=rows[r], in_=y[g][ROWS * r : ROWS * (r + 1), :].rearrange("q (t n) -> q t n", t=PACK)
-                )
-
-        def group_y(g):
-            group_scalar(y_bf[g][:], y_dealt[g][:].rearrange("p (t n) -> p t n", t=PACK))
-
-        def quantize_y(g):
-            quantize(nc, y_codes[g][:], y_scales[:, g, :], y_bf[g][:])
-
-        words = out_1[0].rearrange("p n t -> p (n t)").bitcast(I32)
-
-        def store_words(g):
-            nc.sync.dma_start(
-                out=words[ROWS * g : ROWS * (g + 1), :].rearrange("q (r n) -> r q n", r=4),
-                in_=y_codes[g][:].bitcast(I32),
-            )
-
-        group_scalar(w_bf["f"][:], w_raw["f"][:])
+        regroup_on_scalar(nc, w_bf["f"], w_raw["f"])
         quantize_w("f")
-        nc.vector.tensor_copy(out=walk_out(h_early[:]), in_=walk_in(h_raw[0][:]))
-        quantize(nc, h_codes[:, 0:HALF], h_scales[:, 0:HALF], h_early[:])
-        nc.vector.tensor_copy(out=walk_out(h_late[0][:]), in_=walk_in(h_raw[1][:, :, 0:QUARTER]))
-        group_scalar(h_late[1][:], h_raw[1][:, :, QUARTER:HALF])
-        for u in range(2):
-            cols = slice(HALF + u * QUARTER, HALF + (u + 1) * QUARTER)
-            quantize(nc, h_codes[:, cols], h_scales[:, cols], h_late[u][:])
-        group_scalar(w_bf["c"][:], w_raw["c"][:])
-        group_gpsimd("i")
-        group_gpsimd("o")
+        regroup_on_vector(nc, h_bf_first, h_raw[0])
+        quantize(nc, h_codes[:, 0:HALF], h_scales[:, 0:HALF], h_bf_first)
+        regroup_on_vector(nc, h_bf_last[0], h_raw[1][:, :, 0:QUARTER])
+        regroup_on_scalar(nc, h_bf_last[1], h_raw[1][:, :, QUARTER:HALF])
+        for part in range(2):
+            cols = slice(HALF + part * QUARTER, HALF + (part + 1) * QUARTER)
+            quantize(nc, h_codes[:, cols], h_scales[:, cols], h_bf_last[part])
+        products("f", bank_a)
+
+        for k in ("c", "i"):
+            regroup_on_scalar(nc, w_bf[k], w_raw[k])
         for g in heads:
-            product("f", bank_a, g)
+            add(nc.vector, a_f[g], bank_a[g], x_sb["f"][g])
+            act(tanh_f[g], a_f[g], ACT.Tanh, scale=0.5)
+            act(tanh_shifted[g], a_f[g], ACT.Tanh, bias=0.5 * math.log(2.0), scale=0.5)
+            if g < 2:
+                quantize_w(("c", "i")[g])
+        products("c", bank_b)
+        products("i", bank_a)
         for g in heads:
-            add_x(pre_f, bank_a, "f", g)
-            act(forget, pre_f, ACT.Tanh, g, scale=0.5)
-            s_beta(g)
+            act(log_1s[g], tanh_f[g], ACT.Ln, bias=1.5, scale=0.5)
+
+        regroup_on_vector(nc, w_bf["o"], w_raw["o"])
+        for g in heads:
+            add(nc.vector, a_c[g], bank_b[g], x_sb["c"][g])
             if g == 0:
-                quantize_w("c")
+                quantize_w("o")
+        products("o", bank_b)
         for g in heads:
-            product("c", bank_b, g)
-        for g in heads:
-            act(log_k, forget, ACT.Ln, g, bias=1.5, scale=0.5)
-        for g in heads:
-            add_x(pre_c, bank_b, "c", g)
-        quantize_w("i")
-        quantize_w("o")
-        for g in heads:
-            product("i", bank_a, g)
-        for g in heads:
-            product("o", bank_b, g)
-        for g in heads:
-            v_kept(g)
-        deal(early["pre_c"], pre_c[LAST])
-        deal(early["kept"], kept[LAST])
-        v_part(0)
-        g_pre_a(0)
+            nc.vector.scalar_tensor_tensor(
+                out=kept[g], in0=tanh_shifted[g], scalar=1.0, in1=x_sb["cell"][g], op0=ALU.add, op1=ALU.mult
+            )
+        deal(kept_late, kept, LATE_HEADS, sync_only)
+
+        def start_a_alpha(g):
+            scaled_add(z_less_log[g], log_1s[g], -2.0, bank_a[g])
+            if g < G - 1:
+                add(nc.gpsimd, a_alpha[g], z_less_log[g], x_sb["i"][g])
+
+        start_a_alpha(0)
         for g in heads:
             if g + 1 < G:
-                v_part(g + 1)
-            if g + 1 < LAST:
-                g_pre_a(g + 1)
-            add_x(pre_o, bank_b, "o", g)
-        nc.vector.tensor_tensor(out=pre_a[LAST][:], in0=part_i[LAST][:], in1=x_sb["i"][LAST], op=ALU.add)
-        deal(early["pre_o"], pre_o[LAST])
-        deal(early["pre_a"], pre_a[LAST])
+                start_a_alpha(g + 1)
+            add(nc.vector, a_o[g], bank_b[g], x_sb["o"][g])
+        add(nc.vector, a_alpha[G - 1], z_less_log[G - 1], x_sb["i"][G - 1])
+        deal(a_o_late, a_o, LATE_HEADS, sync_only)
 
-        s_alpha(0)
-        s_cand(0)
-        s_cand(1)
-        s_alpha(1)
-        s_cand(2)
-        s_out(0)
-        s_alpha(2)
-        s_out(1)
-        s_out(2)
-        s_cand(3)
-        s_alpha(3)
-        s_out(3)
+        for g in heads:
+            act(alpha[g], a_alpha[g], ACT.Sigmoid, scale=0.5)
+            act(cand[g], a_c[g], ACT.Tanh)
 
-        v_diff(0)
-        v_diff(1)
-        v_step(0)
-        v_step(1)
-        v_mixed(0)
-        v_diff(2)
-        v_y(0)
-        deal(y_dealt[0], y[0])
-        store_y(0)
-        group_y(0)
-        v_mixed(1)
-        v_step(2)
-        v_y(1)
-        deal(y_dealt[1], y[1])
-        group_y(1)
-        v_mixed(2)
-        v_diff(3, 0)
-        v_y(2)
-        deal(y_dealt[2], y[2])
-        store_y(1)
-        store_y(2)
-        group_y(2)
-        v_diff(3, 1)
-        v_step(3, 0)
-        v_step(3, 1)
-        quantize_y(0)
-        store_words(0)
-        v_mixed(3, 0)
-        v_mixed(3, 1)
-        v_y(3, 0)
-        v_y(3, 1)
-        store_dealt_y(3)
-        for u in range(2):
-            nc.vector.tensor_copy(
-                out=walk_out(y_bf[3][:, u * EIGHTH : (u + 1) * EIGHTH, :]), in_=walk_in(part(y[3], u))
-            )
-        quantize_y(1)
-        store_words(1)
-        quantize_y(3)
-        store_words(3)
-        quantize_y(2)
-        store_words(2)
-        scale_rows = out_2[0].bitcast(I32).rearrange("(g b) (r n) -> r b g n", b=4, r=4)
-        for r in range(4):
-            nc.scalar.dma_start(
-                out=scale_rows[r],
-                in_=y_scales[ROWS * r : ROWS * r + 4, :, :].bitcast(I32),
-            )
+        for pair_heads in (LATE_HEADS, EARLY_HEADS):
+            for g in pair_heads:
+                scaled_add(diff[g], kept[g], -0.25, cand[g])
+            for g in pair_heads:
+                multiply(step[g], diff[g], alpha[g])
+        deal(step_late, step, LATE_HEADS, both_queues)
+        for g in EARLY_HEADS:
+            act(gate_o[g], a_o[g], ACT.Sigmoid)
+        act(gate_o_late, a_o_late, ACT.Sigmoid)
+
+        for g in EARLY_HEADS:
+            scaled_add(mixed[g], kept[g], 0.25, step[g])
+        for g in EARLY_HEADS:
+            multiply(y[g], mixed[g], gate_o[g])
+        deal(y_early, y, EARLY_HEADS, both_queues)
+        for g in EARLY_HEADS:
+            nc.sync.dma_start(out=out_0[M * g : M * (g + 1), :], in_=y[g])
+
+        for out, a, b in zip(column_halves(mixed_late), column_halves(kept_late), column_halves(step_late)):
+            scaled_add(out, a, 0.25, b)
+        for out, a, b in zip(column_halves(y_late), column_halves(mixed_late), column_halves(gate_o_late)):
+            multiply(out, a, b)
+
+        regroup_on_scalar(nc, y_bf[0][:, 0:QUARTER, :], y_late[:, :, 0:QUARTER])
+        late_rows = out_0[0 : 2 * M, :].rearrange("(q t) (half n) -> half q t n", t=PACK, half=2)
+        for half, queue in enumerate(both_queues):
+            queue.dma_start(out=late_rows[half], in_=y_late[2 * ROWS * half : 2 * ROWS * (half + 1), :, :])
+        regroup_on_vector(nc, y_bf[0][:, QUARTER:HALF, :], y_late[:, :, QUARTER:HALF])
+        regroup_on_scalar(nc, y_bf[1][:, 0:QUARTER, :], y_early[:, :, 0:QUARTER])
+        regroup_on_vector(nc, y_bf[1][:, QUARTER:HALF, :], y_early[:, :, QUARTER:HALF])
+        for pair in range(2):
+            quantize(nc, y_codes[:, pair, :], y_scales[:, pair, :], y_bf[pair])
+
+        words = out_1[0].rearrange("p n t -> p (n t)").bitcast(I32)
+        words = words.rearrange("(pair jq) (half n) -> half jq pair n", pair=2, half=2)
+        scale_rows = out_2[0].bitcast(I32).rearrange("(pair j b) (half n) -> half j b pair n", pair=2, j=2, half=2)
+        for half, queue in enumerate(both_queues):
+            queue.dma_start(out=words[half], in_=y_codes[2 * ROWS * half : 2 * ROWS * (half + 1), :, :].bitcast(I32))
+            for j in range(2):
+                first = 2 * ROWS * half + ROWS * j
+                queue.dma_start(out=scale_rows[half][j], in_=y_scales[first : first + SCALE_ROWS, :, :].bitcast(I32))

@@ -60,6 +60,10 @@ def tile_rows_pl_cell_slstm_kernel(tc, h, wi, wf, wo, wc, xi, xf, xo, xc, c, out
         def natural_tiles(name, which):
             return {g: sb.tile([P, N], F32, name="%s%d" % (name, g))[:] for g in which}
 
+        def pair_tiles(name):
+            pairs = [sb.tile([P, 2, N], F32, name="%s%d" % (name, pair))[:] for pair in range(2)]
+            return pairs, [pairs[g // 2][:, g % 2, :] for g in heads]
+
         def dealt_tile(name):
             return sb.tile([P, PACK, HALF], F32, name=name)[:]
 
@@ -80,15 +84,27 @@ def tile_rows_pl_cell_slstm_kernel(tc, h, wi, wf, wo, wc, xi, xf, xo, xc, c, out
         h_codes = sb.tile([P, N], U32, name="h_codes", align_bytes=64)[:]
         h_scales = sb.tile([P, N], U8, name="h_scales", align_bytes=64)[:]
 
-        x_dram = {"f": xf, "c": xc, "i": xi, "o": xo, "cell": c}
-        x_pair = {k: [sb.tile([P, 2, N], F32, name="x_%s%d" % (k, pair))[:] for pair in range(2)] for k in x_dram}
-        x_sb = {k: [x_pair[k][g // 2][:, g % 2, :] for g in heads] for k in x_dram}
+        x_dram = {"f": xf, "c": xc, "o": xo, "cell": c}
+        x_tiles = {k: pair_tiles("x_" + k) for k in x_dram}
+        x_pair = {k: x_tiles[k][0] for k in x_tiles}
+        x_sb = {k: x_tiles[k][1] for k in x_tiles}
+        xi_late = sb.tile([P, 2, N], F32, name="xi_late")[:]
+        xi_early = natural_tiles("xi_early", EARLY_HEADS)
+        xi_sb = [xi_late[:, 0, :], xi_late[:, 1, :], xi_early[2], xi_early[3]]
 
-        a_f, a_c, a_o = (natural_tiles(name, heads) for name in ("a_f", "a_c", "a_o"))
-        tanh_f, tanh_shifted, log_1s = (natural_tiles(name, heads) for name in ("tanh_f", "tanh_shifted", "log_1s"))
-        z_less_log, a_alpha, alpha = (natural_tiles(name, heads) for name in ("z_less_log", "a_alpha", "alpha"))
-        kept, cand, diff, step = (natural_tiles(name, heads) for name in ("kept", "cand", "diff", "step"))
-        gate_o, mixed, y = (natural_tiles(name, EARLY_HEADS) for name in ("gate_o", "mixed", "y"))
+        tanh_f, log_1s, z_less_log = (natural_tiles(name, heads) for name in ("tanh_f", "log_1s", "z_less_log"))
+        a_f_pair, a_f = pair_tiles("a_f")
+        a_c_pair, a_c = pair_tiles("a_c")
+        a_o_pair, a_o = pair_tiles("a_o")
+        a_alpha_pair, a_alpha = pair_tiles("a_alpha")
+        alpha_pair, alpha = pair_tiles("alpha")
+        tanh_shifted_pair, tanh_shifted = pair_tiles("tanh_shifted")
+        kept_pair, kept = pair_tiles("kept")
+        cand_pair, cand = pair_tiles("cand")
+        diff_pair, diff = pair_tiles("diff")
+        step_pair, step = pair_tiles("step")
+        gate_o_early = sb.tile([P, 2, N], F32, name="gate_o_early")[:]
+        mixed, y = (natural_tiles(name, EARLY_HEADS) for name in ("mixed", "y"))
         kept_late, a_o_late, step_late = (dealt_tile(name) for name in ("kept_late", "a_o_late", "step_late"))
         gate_o_late, mixed_late, y_late = (dealt_tile(name) for name in ("gate_o_late", "mixed_late", "y_late"))
         y_early = dealt_tile("y_early")
@@ -146,15 +162,18 @@ def tile_rows_pl_cell_slstm_kernel(tc, h, wi, wf, wo, wc, xi, xf, xo, xc, c, out
             nc.sync.dma_start(out=h_raw[half], in_=h_rows[:, :, half * HALF : (half + 1) * HALF])
         load_x("f", 0)
         load_w("c")
-        load_w("i")
         load_x("f", 1)
+        load_x("c", 0)
+        load_x("c", 1)
+        load_w("i")
+        load_x("cell", 0)
         load_w("o")
-        for k in ("c", "cell"):
-            for pair in range(2):
-                load_x(k, pair)
-        for pair in range(2):
-            load_x("i", pair)
-            load_x("o", pair)
+        nc.sync.dma_start(out=xi_late, in_=xi[0:2].rearrange("g m n -> m g n"))
+        load_x("o", 0)
+        nc.sync.dma_start(out=xi_early[2], in_=xi[2])
+        load_x("o", 1)
+        nc.sync.dma_start(out=xi_early[3], in_=xi[3])
+        load_x("cell", 1)
 
         regroup_on_scalar(nc, w_bf["f"], w_raw["f"])
         quantize_w("f")
@@ -167,62 +186,74 @@ def tile_rows_pl_cell_slstm_kernel(tc, h, wi, wf, wo, wc, xi, xf, xo, xc, c, out
             quantize(nc, h_codes[:, cols], h_scales[:, cols], h_bf_last[part])
         products("f", bank_a)
 
-        for k in ("c", "i"):
-            regroup_on_scalar(nc, w_bf[k], w_raw[k])
+        def shifted_tanh(out, in_):
+            act(out, in_, ACT.Tanh, bias=0.5 * math.log(2.0), scale=0.5)
+
+        def make_kept(pair):
+            nc.vector.scalar_tensor_tensor(
+                out=kept_pair[pair].rearrange("p g n -> p (g n)"),
+                in0=tanh_shifted_pair[pair].rearrange("p g n -> p (g n)"),
+                scalar=1.0,
+                in1=x_pair["cell"][pair].rearrange("p g n -> p (g n)"),
+                op0=ALU.add,
+                op1=ALU.mult,
+            )
+
+        regroup_on_scalar(nc, w_bf["c"], w_raw["c"])
         for g in heads:
             add(nc.vector, a_f[g], bank_a[g], x_sb["f"][g])
             act(tanh_f[g], a_f[g], ACT.Tanh, scale=0.5)
-            act(tanh_shifted[g], a_f[g], ACT.Tanh, bias=0.5 * math.log(2.0), scale=0.5)
-            if g < 2:
-                quantize_w(("c", "i")[g])
+            if g in LATE_HEADS:
+                shifted_tanh(tanh_shifted[g], a_f[g])
+            if g == 0:
+                quantize_w("c")
         products("c", bank_b)
-        products("i", bank_a)
         for g in heads:
             act(log_1s[g], tanh_f[g], ACT.Ln, bias=1.5, scale=0.5)
 
-        regroup_on_vector(nc, w_bf["o"], w_raw["o"])
         for g in heads:
+            if g == G - 1:
+                regroup_on_vector(nc, w_bf["i"], w_raw["i"])
             add(nc.vector, a_c[g], bank_b[g], x_sb["c"][g])
+        quantize_w("i")
+        products("i", bank_a)
+        make_kept(0)
+        deal(kept_late, kept, LATE_HEADS, sync_only)
+        regroup_on_vector(nc, w_bf["o"], w_raw["o"])
+
+        for g in heads:
+            scaled_add(z_less_log[g], log_1s[g], -2.0, bank_a[g])
             if g == 0:
                 quantize_w("o")
+            if g < G - 1:
+                add(nc.gpsimd, a_alpha[g], z_less_log[g], xi_sb[g])
         products("o", bank_b)
         for g in heads:
-            nc.vector.scalar_tensor_tensor(
-                out=kept[g], in0=tanh_shifted[g], scalar=1.0, in1=x_sb["cell"][g], op0=ALU.add, op1=ALU.mult
-            )
-        deal(kept_late, kept, LATE_HEADS, sync_only)
-
-        def start_a_alpha(g):
-            scaled_add(z_less_log[g], log_1s[g], -2.0, bank_a[g])
-            if g < G - 1:
-                add(nc.gpsimd, a_alpha[g], z_less_log[g], x_sb["i"][g])
-
-        start_a_alpha(0)
-        for g in heads:
-            if g + 1 < G:
-                start_a_alpha(g + 1)
             add(nc.vector, a_o[g], bank_b[g], x_sb["o"][g])
-        add(nc.vector, a_alpha[G - 1], z_less_log[G - 1], x_sb["i"][G - 1])
+        add(nc.vector, a_alpha[G - 1], z_less_log[G - 1], xi_sb[G - 1])
         deal(a_o_late, a_o, LATE_HEADS, sync_only)
 
-        for g in heads:
-            act(alpha[g], a_alpha[g], ACT.Sigmoid, scale=0.5)
-            act(cand[g], a_c[g], ACT.Tanh)
-
-        for pair_heads in (LATE_HEADS, EARLY_HEADS):
-            for g in pair_heads:
-                scaled_add(diff[g], kept[g], -0.25, cand[g])
-            for g in pair_heads:
-                multiply(step[g], diff[g], alpha[g])
+        act(alpha[0], a_alpha[0], ACT.Sigmoid, scale=0.5)
+        act(cand_pair[0], a_c_pair[0], ACT.Tanh)
+        shifted_tanh(tanh_shifted_pair[1], a_f_pair[1])
+        act(alpha[1], a_alpha[1], ACT.Sigmoid, scale=0.5)
+        act(cand_pair[1], a_c_pair[1], ACT.Tanh)
+        scaled_add(diff_pair[0], kept_pair[0], -0.25, cand_pair[0])
+        make_kept(1)
+        multiply(step_pair[0], diff_pair[0], alpha_pair[0])
+        act(alpha_pair[1], a_alpha_pair[1], ACT.Sigmoid, scale=0.5)
         deal(step_late, step, LATE_HEADS, both_queues)
         for g in EARLY_HEADS:
-            act(gate_o[g], a_o[g], ACT.Sigmoid)
+            scaled_add(diff[g], kept[g], -0.25, cand[g])
+        for g in EARLY_HEADS:
+            multiply(step[g], diff[g], alpha[g])
+        act(gate_o_early, a_o_pair[1], ACT.Sigmoid)
         act(gate_o_late, a_o_late, ACT.Sigmoid)
 
         for g in EARLY_HEADS:
             scaled_add(mixed[g], kept[g], 0.25, step[g])
         for g in EARLY_HEADS:
-            multiply(y[g], mixed[g], gate_o[g])
+            multiply(y[g], mixed[g], gate_o_early[:, g % 2, :])
         deal(y_early, y, EARLY_HEADS, both_queues)
         for g in EARLY_HEADS:
             nc.sync.dma_start(out=out_0[M * g : M * (g + 1), :], in_=y[g])

import math
from contextlib import ExitStack

import concourse.mybir as mybir

G, D, M, N = 4, 128, 128, 512
FLOPS = 2 * 4 * G * D * M * N

F32 = mybir.dt.float32
BF16 = mybir.dt.bfloat16
I32 = mybir.dt.int32
U32 = mybir.dt.uint32
U8 = mybir.dt.uint8
FP8X4 = mybir.dt.float8_e4m3fn_x4
ALU = mybir.AluOpType
ACT = mybir.ActivationFunctionType

P = 128
PACK = 4
ROWS = D // PACK
SCALE_ROWS = 4
RUN = 4
HALF = N // 2
QUARTER = N // 4
LATE_HEADS = (0, 1)
EARLY_HEADS = (2, 3)


def quantize(nc, codes, scales, grouped):
    nc.vector.quantize_mx(
        out=codes.bitcast(FP8X4), scales=scales, in_=grouped.rearrange("p c t -> p (c t)")
    )


def regroup_views(grouped, raw):
    return (
        grouped.rearrange("p (c i) t -> p c t i", i=RUN),
        raw.rearrange("p t (c i) -> p c t i", i=RUN),
    )


def regroup_on_scalar(nc, grouped, raw):
    out, in_ = regroup_views(grouped, raw)
    nc.scalar.activation(out=out, in_=in_, func=ACT.Copy)


def regroup_on_vector(nc, grouped, raw):
    out, in_ = regroup_views(grouped, raw)
    nc.vector.tensor_copy(out=out, in_=in_)


def tile_rows_pl_cell_slstm_kernel(tc, h, wi, wf, wo, wc, xi, xf, xo, xc, c, out_0, out_1, out_2):
    nc = tc.nc
    heads = range(G)
    with ExitStack() as ctx:
        sb = ctx.enter_context(tc.tile_pool(name="sb", bufs=1))
        psum = ctx.enter_context(tc.psum_pool(name="psum", bufs=1))
        ctx.enter_context(tc.manual_schedule())

        def natural_tiles(name, which):
            return {g: sb.tile([P, N], F32, name="%s%d" % (name, g))[:] for g in which}

        def pair_tiles(name):
            pairs = [sb.tile([P, 2, N], F32, name="%s%d" % (name, pair))[:] for pair in range(2)]
            return pairs, [pairs[g // 2][:, g % 2, :] for g in heads]

        def dealt_tile(name):
            return sb.tile([P, PACK, HALF], F32, name=name)[:]

        def column_halves(dealt):
            return [dealt[:, :, 0:QUARTER], dealt[:, :, QUARTER:HALF]]

        bank_a = [psum.tile([M, N], F32, name="bank_a%d" % g)[:] for g in heads]
        bank_b = [psum.tile([M, N], F32, name="bank_b%d" % g)[:] for g in heads]

        w_dram = {"f": wf, "c": wc, "i": wi, "o": wo}
        w_raw = {k: sb.tile([P, PACK, M], F32, name="w_raw_" + k)[:] for k in w_dram}
        w_bf = {k: sb.tile([P, M, PACK], BF16, name="w_bf_" + k, align_bytes=64)[:] for k in w_dram}
        w_codes = {k: sb.tile([P, M], U32, name="w_codes_" + k, align_bytes=64)[:] for k in w_dram}
        w_scales = {k: sb.tile([P, M], U8, name="w_scales_" + k, align_bytes=64)[:] for k in w_dram}
        h_raw = [sb.tile([P, PACK, HALF], F32, name="h_raw%d" % half)[:] for half in range(2)]
        h_bf_first = sb.tile([P, HALF, PACK], BF16, name="h_bf_first", align_bytes=64)[:]
        h_bf_last = [sb.tile([P, QUARTER, PACK], BF16, name="h_bf_last%d" % part, align_bytes=64)[:] for part in range(2)]
        h_codes = sb.tile([P, N], U32, name="h_codes", align_bytes=64)[:]
        h_scales = sb.tile([P, N], U8, name="h_scales", align_bytes=64)[:]

        x_dram = {"f": xf, "c": xc, "o": xo, "cell": c}
        x_tiles = {k: pair_tiles("x_" + k) for k in x_dram}
        x_pair = {k: x_tiles[k][0] for k in x_tiles}
        x_sb = {k: x_tiles[k][1] for k in x_tiles}
        xi_late = sb.tile([P, 2, N], F32, name="xi_late")[:]
        xi_early = natural_tiles("xi_early", EARLY_HEADS)
        xi_sb = [xi_late[:, 0, :], xi_late[:, 1, :], xi_early[2], xi_early[3]]

        tanh_f, log_1s, z_less_log = (natural_tiles(name, heads) for name in ("tanh_f", "log_1s", "z_less_log"))
        a_f_pair, a_f = pair_tiles("a_f")
        a_c_pair, a_c = pair_tiles("a_c")
        a_o_pair, a_o = pair_tiles("a_o")
        a_alpha_pair, a_alpha = pair_tiles("a_alpha")
        alpha_pair, alpha = pair_tiles("alpha")
        tanh_shifted_pair, tanh_shifted = pair_tiles("tanh_shifted")
        kept_pair, kept = pair_tiles("kept")
        cand_pair, cand = pair_tiles("cand")
        diff_pair, diff = pair_tiles("diff")
        step_pair, step = pair_tiles("step")
        gate_o_early = sb.tile([P, 2, N], F32, name="gate_o_early")[:]
        mixed, y = (natural_tiles(name, EARLY_HEADS) for name in ("mixed", "y"))
        kept_late, a_o_late, step_late = (dealt_tile(name) for name in ("kept_late", "a_o_late", "step_late"))
        gate_o_late, mixed_late, y_late = (dealt_tile(name) for name in ("gate_o_late", "mixed_late", "y_late"))
        y_early = dealt_tile("y_early")
        y_bf = [sb.tile([P, HALF, PACK], BF16, name="y_bf%d" % pair, align_bytes=64)[:] for pair in range(2)]
        y_codes = sb.tile([P, 2, HALF], U32, name="y_codes", align_bytes=64)[:]
        y_scales = sb.tile([P, 2, HALF], U8, name="y_scales", align_bytes=64)[:]

        def load_w(k):
            nc.sync.dma_start(out=w_raw[k], in_=w_dram[k].rearrange("g (p t) m -> (g p) t m", t=PACK))

        def load_x(k, pair):
            nc.sync.dma_start(out=x_pair[k][pair], in_=x_dram[k][2 * pair : 2 * pair + 2].rearrange("g m n -> m g n"))

        def quantize_w(k):
            quantize(nc, w_codes[k], w_scales[k], w_bf[k])

        def products(k, bank):
            for g in heads:
                rows = slice(ROWS * g, ROWS * (g + 1))
                nc.tensor.matmul_mx(
                    out=bank[g],
                    lhsT=w_codes[k][rows, :].bitcast(FP8X4),
                    lhsT_scale=w_scales[k][rows, :],
                    rhs=h_codes[rows, :].bitcast(FP8X4),
                    rhs_scale=h_scales[rows, :],
                    start=True,
                    stop=True,
                )

        def act(out, in_, func, bias=0.0, scale=1.0):
            nc.scalar.activation(out=out, in_=in_, func=func, bias=bias, scale=scale)

        def add(engine, out, a, b):
            engine.tensor_tensor(out=out, in0=a, in1=b, op=ALU.add)

        def multiply(out, a, b):
            nc.vector.tensor_tensor(out=out, in0=a, in1=b, op=ALU.mult)

        def scaled_add(out, a, factor, b):
            nc.vector.scalar_tensor_tensor(out=out, in0=a, scalar=factor, in1=b, op0=ALU.mult, op1=ALU.add)

        def deal(dealt, natural, pair_heads, queues):
            for g in pair_heads:
                for half, queue in enumerate(queues):
                    first = 2 * ROWS * half + ROWS * (g % 2)
                    queue.dma_start(
                        out=dealt[first : first + ROWS, :, :], in_=natural[g][:, HALF * half : HALF * (half + 1)]
                    )

        sync_only, both_queues = (nc.sync, nc.sync), (nc.sync, nc.scalar)

        h_rows = h.rearrange("g (p t) n -> (g p) t n", t=PACK)
        load_w("f")
        for half in range(2):
            nc.sync.dma_start(out=h_raw[half], in_=h_rows[:, :, half * HALF : (half + 1) * HALF])
        load_x("f", 0)
        load_w("c")
        load_x("f", 1)
        load_x("c", 0)
        load_x("c", 1)
        load_w("i")
        load_x("cell", 0)
        load_w("o")
        nc.sync.dma_start(out=xi_late, in_=xi[0:2].rearrange("g m n -> m g n"))
        load_x("o", 0)
        nc.sync.dma_start(out=xi_early[2], in_=xi[2])
        load_x("o", 1)
        nc.sync.dma_start(out=xi_early[3], in_=xi[3])
        load_x("cell", 1)

        regroup_on_scalar(nc, w_bf["f"], w_raw["f"])
        quantize_w("f")
        regroup_on_vector(nc, h_bf_first, h_raw[0])
        quantize(nc, h_codes[:, 0:HALF], h_scales[:, 0:HALF], h_bf_first)
        regroup_on_vector(nc, h_bf_last[0], h_raw[1][:, :, 0:QUARTER])
        regroup_on_scalar(nc, h_bf_last[1], h_raw[1][:, :, QUARTER:HALF])
        for part in range(2):
            cols = slice(HALF + part * QUARTER, HALF + (part + 1) * QUARTER)
            quantize(nc, h_codes[:, cols], h_scales[:, cols], h_bf_last[part])
        products("f", bank_a)

        def shifted_tanh(out, in_):
            act(out, in_, ACT.Tanh, bias=0.5 * math.log(2.0), scale=0.5)

        def make_kept(pair):
            nc.vector.scalar_tensor_tensor(
                out=kept_pair[pair].rearrange("p g n -> p (g n)"),
                in0=tanh_shifted_pair[pair].rearrange("p g n -> p (g n)"),
                scalar=1.0,
                in1=x_pair["cell"][pair].rearrange("p g n -> p (g n)"),
                op0=ALU.add,
                op1=ALU.mult,
            )

        regroup_on_scalar(nc, w_bf["c"], w_raw["c"])
        for g in heads:
            add(nc.vector, a_f[g], bank_a[g], x_sb["f"][g])
            act(tanh_f[g], a_f[g], ACT.Tanh, scale=0.5)
            if g in LATE_HEADS:
                shifted_tanh(tanh_shifted[g], a_f[g])
            if g == 0:
                quantize_w("c")
        products("c", bank_b)
        for g in heads:
            act(log_1s[g], tanh_f[g], ACT.Ln, bias=1.5, scale=0.5)

        for g in heads:
            if g == G - 1:
                regroup_on_vector(nc, w_bf["i"], w_raw["i"])
            add(nc.vector, a_c[g], bank_b[g], x_sb["c"][g])
        quantize_w("i")
        products("i", bank_a)
        make_kept(0)
        deal(kept_late, kept, LATE_HEADS, sync_only)
        regroup_on_vector(nc, w_bf["o"], w_raw["o"])

        for g in heads:
            scaled_add(z_less_log[g], log_1s[g], -2.0, bank_a[g])
            if g == 0:
                quantize_w("o")
            if g < G - 1:
                add(nc.gpsimd, a_alpha[g], z_less_log[g], xi_sb[g])
        products("o", bank_b)
        for g in heads:
            add(nc.vector, a_o[g], bank_b[g], x_sb["o"][g])
        add(nc.vector, a_alpha[G - 1], z_less_log[G - 1], xi_sb[G - 1])
        deal(a_o_late, a_o, LATE_HEADS, sync_only)

        act(alpha[0], a_alpha[0], ACT.Sigmoid, scale=0.5)
        act(cand_pair[0], a_c_pair[0], ACT.Tanh)
        shifted_tanh(tanh_shifted_pair[1], a_f_pair[1])
        act(alpha[1], a_alpha[1], ACT.Sigmoid, scale=0.5)
        act(cand_pair[1], a_c_pair[1], ACT.Tanh)
        scaled_add(diff_pair[0], kept_pair[0], -0.25, cand_pair[0])
        make_kept(1)
        multiply(step_pair[0], diff_pair[0], alpha_pair[0])
        act(alpha_pair[1], a_alpha_pair[1], ACT.Sigmoid, scale=0.5)
        deal(step_late, step, LATE_HEADS, both_queues)
        for g in EARLY_HEADS:
            scaled_add(diff[g], kept[g], -0.25, cand[g])
        for g in EARLY_HEADS:
            multiply(step[g], diff[g], alpha[g])
        act(gate_o_early, a_o_pair[1], ACT.Sigmoid)
        act(gate_o_late, a_o_late, ACT.Sigmoid)

        for g in EARLY_HEADS:
            scaled_add(mixed[g], kept[g], 0.25, step[g])
        for g in EARLY_HEADS:
            multiply(y[g], mixed[g], gate_o_early[:, g % 2, :])
        deal(y_early, y, EARLY_HEADS, both_queues)
        for g in EARLY_HEADS:
            nc.sync.dma_start(out=out_0[M * g : M * (g + 1), :], in_=y[g])

        for out, a, b in zip(column_halves(mixed_late), column_halves(kept_late), column_halves(step_late)):
            scaled_add(out, a, 0.25, b)
        for out, a, b in zip(column_halves(y_late), column_halves(mixed_late), column_halves(gate_o_late)):
            multiply(out, a, b)

        regroup_on_scalar(nc, y_bf[0][:, 0:QUARTER, :], y_late[:, :, 0:QUARTER])
        late_rows = out_0[0 : 2 * M, :].rearrange("(q t) (half n) -> half q t n", t=PACK, half=2)
        for half, queue in enumerate(both_queues):
            queue.dma_start(out=late_rows[half], in_=y_late[2 * ROWS * half : 2 * ROWS * (half + 1), :, :])
        regroup_on_vector(nc, y_bf[0][:, QUARTER:HALF, :], y_late[:, :, QUARTER:HALF])
        regroup_on_scalar(nc, y_bf[1][:, 0:QUARTER, :], y_early[:, :, 0:QUARTER])
        regroup_on_vector(nc, y_bf[1][:, QUARTER:HALF, :], y_early[:, :, QUARTER:HALF])
        for pair in range(2):
            quantize(nc, y_codes[:, pair, :], y_scales[:, pair, :], y_bf[pair])

        words = out_1[0].rearrange("p n t -> p (n t)").bitcast(I32)
        words = words.rearrange("(pair jq) (half n) -> half jq pair n", pair=2, half=2)
        scale_rows = out_2[0].bitcast(I32).rearrange("(pair j b) (half n) -> half j b pair n", pair=2, j=2, half=2)
        for half, queue in enumerate(both_queues):
            queue.dma_start(out=words[half], in_=y_codes[2 * ROWS * half : 2 * ROWS * (half + 1), :, :].bitcast(I32))
            for j in range(2):
                first = 2 * ROWS * half + ROWS * j
                queue.dma_start(out=scale_rows[half][j], in_=y_scales[first : first + SCALE_ROWS, :, :].bitcast(I32))
